import numpy as np
import ml_dtypes


def mxq(x, axis, fmt="e4m3"):
    dtype, down = {"e4m3": (ml_dtypes.float8_e4m3fn, 7), "e5m2": (ml_dtypes.float8_e5m2, 14)}[fmt]
    v = np.moveaxis(np.asarray(x, np.float32).astype(ml_dtypes.bfloat16).astype(np.float64), axis, -1)
    blocks = v.reshape(v.shape[:-1] + (-1, 32))
    amax = np.abs(blocks).max(-1, keepdims=True)
    byte = np.maximum(np.where(amax > 0, np.frexp(amax)[1] - 1 + 127, 0) - down, 1)
    scale = np.exp2(byte - 127.0)
    codes = (blocks / scale).astype(np.float32).astype(dtype).astype(np.float64)
    return np.moveaxis((codes * scale).reshape(v.shape), -1, axis)


WIDE = False


def mx_kscale(k):
    if not WIDE:
        return np.ones(k)
    levels = np.array([30, -30])
    if k % 512:
        return np.exp2(np.random.permutation(np.resize(levels, k // 32))).repeat(32)
    a = np.empty((k // 512, 16))
    for p in range(k // 512):
        a[p, :8] = np.random.permutation(np.resize(levels, 8))
        for g in range(8):
            far = levels[np.abs(levels - a[p, g]) >= 10]
            a[p, g + 8] = far[np.random.randint(len(far))]
    return np.exp2(a.ravel()).repeat(32)


def f64(x):
    return np.asarray(x).astype(np.float64)


def striped(idx):
    return np.tile(np.asarray(idx).reshape(-1, 16).T, (8, 1)).astype(np.uint16)


def unstriped(offs):
    return offs[:16].T.reshape(-1).astype(np.int64)


E2M1 = np.array([0.0, 0.5, 1.0, 1.5, 2.0, 3.0, 4.0, 6.0, -0.0, -0.5, -1.0, -1.5, -2.0, -3.0, -4.0, -6.0])


def pack_weight(w, fmt):
    k, n = w.shape
    w = f64(np.asarray(w, np.float32).astype(ml_dtypes.bfloat16)).reshape(k // 32, 32, n)
    amax = np.abs(w).max(1)
    if fmt in ("e4m3", "e5m2"):
        byte = np.frexp(amax)[1] - 1 + 127 - (7 if fmt == "e4m3" else 14)
    else:
        mant, ex = np.frexp(amax / 6.0)
        byte = np.where(mant > 0.5, ex, ex - 1) + 127
    byte = np.clip(np.where(amax > 0, byte, 1), 1, 254)
    scaled = (w * np.exp2(127.0 - byte)[:, None, :]).reshape(k, n).astype(np.float32)
    by_word = np.ascontiguousarray(scaled.reshape(k // 512, 128, 4, n).transpose(0, 1, 3, 2))
    if fmt in ("e4m3", "e5m2"):
        words = by_word.astype(ml_dtypes.float8_e4m3fn if fmt == "e4m3" else ml_dtypes.float8_e5m2).view(np.uint8)
    else:
        c = by_word.astype(ml_dtypes.float4_e2m1fn).view(np.uint8) & 0xF
        words = (c[..., 0::2] | (c[..., 1::2] << 4)).reshape(k // 512, 128, 2 * n)
    return np.ascontiguousarray(words), np.ascontiguousarray(byte.astype(np.uint8).reshape(k // 512, 16, n))


def unpack_weight(words, scales, fmt):
    g, _, n = scales.shape
    words = np.ascontiguousarray(words).reshape(g, 128, n, -1)
    if fmt in ("e4m3", "e5m2"):
        vals = words.view(ml_dtypes.float8_e4m3fn if fmt == "e4m3" else ml_dtypes.float8_e5m2).astype(np.float64)
    else:
        nib = np.empty((g, 128, n, 4), np.uint8)
        nib[..., 0::2] = words & 0xF
        nib[..., 1::2] = words >> 4
        vals = E2M1[nib]
    vals = vals * np.repeat(np.exp2(scales.astype(np.float64) - 127.0), 8, axis=1)[..., None]
    return vals.transpose(0, 1, 3, 2).reshape(g * 512, n)


def sigmoid(v):
    return 1.0 / (1.0 + np.exp(-v))


def sgn(shape):
    return np.random.uniform(0.5, 2.0, shape) * np.where(np.random.standard_normal(shape) < 0, -1.0, 1.0)


K, T, J, R, F, Z, N, C, O = 512, 1024, 256, 512, 512, 1024, 256, 512, 128


def setup_inputs():
    n = np.random.standard_normal
    idx = np.random.permutation(T)[:J]
    idx2 = np.random.permutation(Z)[:J]
    idx3 = np.random.permutation(C)[:J]
    idx4 = np.random.permutation(C)[:O]
    idx5 = np.random.permutation(C)[:O]
    idx6 = np.random.permutation(J)[:O]
    fk = mx_kscale(K)
    ff = mx_kscale(F)
    fr = mx_kscale(R)
    xtp = pack_weight(n((K, T)) / fk[:, None], "e2m1")
    xop = pack_weight(n((F, Z)) / ff[:, None], "e5m2")
    wp = pack_weight(n((K, R)) * 1 / np.sqrt(K) * fk[:, None] * fr, "e5m2")
    w0p = pack_weight(n((F, R)) * 1 / np.sqrt(F) * ff[:, None] * fr, "e4m3")
    w2p = pack_weight(n((F, R)) * 1 / np.sqrt(F) * ff[:, None] * fr, "e4m3")
    wbp = pack_weight(n((R, N)) * 1 / np.sqrt(R) / fr[:, None], "e4m3")
    wcp = pack_weight(n((R, N)) * 1 / np.sqrt(R) / fr[:, None], "e2m1")
    return {
        "xt_words": xtp[0],
        "xt_scales": xtp[1],
        "xo_words": xop[0],
        "xo_scales": xop[1],
        "w_words": wp[0],
        "w_scales": wp[1],
        "w0_words": w0p[0],
        "w0_scales": w0p[1],
        "w2_words": w2p[0],
        "w2_scales": w2p[1],
        "wb_words": wbp[0],
        "wb_scales": wbp[1],
        "wc_words": wcp[0],
        "wc_scales": wcp[1],
        "so": (np.random.uniform(0.5, 1.6, (N, 1))).astype(np.float32),
        "sp": (sgn((N, 1))).astype(np.float32),
        "bo": (np.random.uniform(-2.0, 2.0, (N, 1))).astype(np.float32),
        "offs": striped(idx),
        "offs2": striped(idx2),
        "offs3": striped(idx3),
        "offs4": striped(idx4),
        "offs5": striped(idx5),
        "offs6": striped(idx6),
    }


def reference(xt_words, xt_scales, xo_words, xo_scales, w_words, w_scales, w0_words, w0_scales, w2_words, w2_scales, wb_words, wb_scales, wc_words, wc_scales, so, sp, bo, offs, offs2, offs3, offs4, offs5, offs6):
    idx = unstriped(offs)
    idx2 = unstriped(offs2)
    idx3 = unstriped(offs3)
    idx4 = unstriped(offs4)
    idx5 = unstriped(offs5)
    idx6 = unstriped(offs6)
    xtu = unpack_weight(xt_words, xt_scales, "e2m1")
    xou = unpack_weight(xo_words, xo_scales, "e5m2")
    wu = unpack_weight(w_words, w_scales, "e5m2")
    w0u = unpack_weight(w0_words, w0_scales, "e4m3")
    w2u = unpack_weight(w2_words, w2_scales, "e4m3")
    wbu = unpack_weight(wb_words, wb_scales, "e4m3")
    wcu = unpack_weight(wc_words, wc_scales, "e2m1")
    xtidxg = xtu[:, idx]
    xoidx2g = xou[:, idx2]
    a = wu.T @ xtidxg + w0u.T @ xoidx2g
    b = w2u.T @ xoidx2g
    hid = np.abs(a - b)
    hidq = mxq(hid, 0, "e5m2")
    p = wbu.T @ hidq
    q = wcu.T @ hidq
    pw = np.zeros((N, C))
    pw[:, idx3] = p
    y = pw[:, idx4] * f64(so) * sigmoid(pw[:, idx5] * f64(sp) + f64(bo)) - q[:, idx6]
    return y

@@ -1,0 +1,225 @@
+from contextlib import ExitStack
+
+import concourse.mybir as mybir
+
+K, T, J, R, F, Z, N, C, O = 512, 1024, 256, 512, 512, 1024, 256, 512, 128
+FLOPS = 2 * (3 * 512 * R * J + 2 * R * N * J)
+
+F32, BF16 = mybir.dt.float32, mybir.dt.bfloat16
+I32, U32, U16, U8 = mybir.dt.int32, mybir.dt.uint32, mybir.dt.uint16, mybir.dt.uint8
+E4M3, E5M2, E2M1 = mybir.dt.float8_e4m3fn_x4, mybir.dt.float8_e5m2_x4, mybir.dt.float4_e2m1fn_x4
+ACT = mybir.ActivationFunctionType
+ALU = mybir.AluOpType
+P = 128
+H = 128
+
+
+def tile_list_outcomegatedboard_noted_kernel(
+    tc, xt_words, xt_scales, xo_words, xo_scales, w_words, w_scales, w0_words, w0_scales, w2_words, w2_scales,
+    wb_words, wb_scales, wc_words, wc_scales, so, sp, bo, offs, offs2, offs3, offs4, offs5, offs6, out,
+):
+    nc = tc.nc
+    with ExitStack() as ctx:
+        lists = ctx.enter_context(tc.tile_pool(name="lists", bufs=1))
+        sb = ctx.enter_context(tc.tile_pool(name="sb", bufs=1))
+        ps = ctx.enter_context(tc.psum_pool(name="ps", bufs=1))
+
+        def tile(name, shape, dtype, tag=None):
+            return sb.tile(shape, dtype, name=name, tag=tag or name, align_bytes=64)
+
+        def load_list(name, src):
+            dst = lists.tile(list(src.shape), U16, name=name)
+            nc.sync.dma_start(dst[:], src)
+            return dst
+
+        def load_words(name, src, width, dtype):
+            dst = tile(name, [P, width], dtype)
+            flat = src[0] if src.ndim == 3 else src[0].rearrange("p c r -> p (c r)")
+            nc.sync.dma_start(dst[:].bitcast(I32), flat.bitcast(I32))
+            return dst
+
+        def stage_tile(name, width, half):
+            stage = tile(name, [P, 2, width], U8)
+            nc.vector.memset(stage[64 * half : 64 * half + 64].bitcast(I32), 0)
+            return stage
+
+        def stage_scales(stage, src, half):
+            rows = src[0].bitcast(I32).rearrange("(h g r) c -> g r h c", h=2, g=2)
+            for g in range(2):
+                first = 64 * half + 32 * g
+                nc.sync.dma_start(stage[first : first + 4].bitcast(I32), rows[g])
+
+        def spread_into(name, stage, width, half):
+            plane = tile(name, [P, width], U8)
+            for h in range(2):
+                nc.vector.tensor_copy(plane[64 * h : 64 * h + 64].bitcast(I32), stage[64 * half : 64 * half + 64, h].bitcast(I32))
+            return plane
+
+        def quad_tile(name, width):
+            quad = tile(name, [P, 4, width], U8)
+            nc.vector.memset(quad[:, 0].bitcast(I32), 0)
+            return quad
+
+        def load_plane(name, src):
+            plane = tile(name, [P, src.shape[2]], U8)
+            nc.vector.memset(plane[:].bitcast(I32), 0)
+            return plane
+
+        def load_rows(plane, src):
+            for q in range(4):
+                nc.sync.dma_start(plane[32 * q : 32 * q + 4].bitcast(I32), src[0, 4 * q : 4 * q + 4].bitcast(I32))
+
+        def load_quad(quad, src, first=0):
+            rows = src[0].bitcast(I32).rearrange("(q r) c -> r q c", q=4)
+            nc.scalar.dma_start(quad[0:4, :, first : first + src.shape[2]].bitcast(I32), rows)
+
+        def spread_within(quad):
+            for q in range(1, 4):
+                nc.vector.tensor_copy(quad[32 * q : 32 * q + 4, 0].bitcast(I32), quad[0:4, q].bitcast(I32))
+            return quad[:, 0]
+
+        def spread_from(plane, quad):
+            for q in range(4):
+                nc.vector.tensor_copy(plane[32 * q : 32 * q + 4].bitcast(I32), quad[:, q].bitcast(I32))
+
+        def deal_scales(name, plane):
+            dealt = tile(name, [P, 4, P], U8)
+            nc.gpsimd.tensor_copy(dealt[:], plane.rearrange("p (m t) -> p t m", t=4))
+            return dealt
+
+        def deal_words(name, words):
+            dealt = tile(name, [P, 4, P], U32)
+            nc.scalar.copy(dealt[:].rearrange("p t m -> p m t"), words[:].rearrange("p (m t) -> p m t", t=4))
+            return dealt
+
+        def load_column(name, src):
+            dst = tile(name, [P, 2], F32)
+            with nc.allow_non_contiguous_dma(reason="one value a partition"):
+                nc.sync.dma_start(dst[:], src.rearrange("(u p) o -> p (u o)", p=P))
+            return dst
+
+        w_quad = quad_tile("w_quad", R)
+        xo_s = load_plane("xo_s", xo_scales)
+        w2_plane = load_plane("w2_plane", w2_scales)
+        w0_plane = load_plane("w0_plane", w0_scales)
+        xt_stage = stage_tile("xt_stage", T, 1)
+        wb_s = load_plane("wb_s", wb_scales)
+        wc_s = load_plane("wc_s", wc_scales)
+        board = [tile("board%d" % u, [P, C], F32) for u in range(2)]
+        for u in range(2):
+            nc.gpsimd.memset(board[u][:], 0.0)
+
+        xo_quad = tile("xo_quad", [4, 4, Z], U8)
+        load_quad(xo_quad, xo_scales)
+        w2_quad = tile("w2_quad", [4, 4, R], U8)
+        load_quad(w2_quad, w2_scales)
+        w0_quad = tile("w0_quad", [4, 4, R], U8)
+        load_quad(w0_quad, w0_scales)
+        load_quad(w_quad, w_scales)
+        l2 = load_list("l2", offs2)
+        l1 = load_list("l1", offs)
+        w2_w = load_words("w2_w", w2_words, R, U32)
+        xo_w = load_words("xo_w", xo_words, Z, U32)
+        w0_w = load_words("w0_w", w0_words, R, U32)
+        w_w = load_words("w_w", w_words, R, U32)
+        stage_scales(xt_stage, xt_scales, 1)
+        xt_w = load_words("xt_w", xt_words, T, U16)
+        load_rows(wb_s, wb_scales)
+        wb_w = load_words("wb_w", wb_words, N, U32)
+        l3 = load_list("l3", offs3)
+        load_rows(wc_s, wc_scales)
+        wc_w = load_words("wc_w", wc_words, N, U16)
+        l5 = load_list("l5", offs5)
+        l4 = load_list("l4", offs4)
+        l6 = load_list("l6", offs6)
+        sp_c = load_column("sp_c", sp)
+        bo_c = load_column("bo_c", bo)
+        so_c = load_column("so_c", so)
+
+        spread_from(xo_s, xo_quad)
+        spread_from(w2_plane, w2_quad)
+        w2_s = deal_scales("w2_s", w2_plane[:])
+        w2_d = deal_words("w2_d", w2_w)
+        xo_gs = tile("xo_gs", [P, J], U8)
+        nc.vector.tensor_copy(xo_gs[:], xo_s[:].indirect(l2[:]))
+        spread_from(w0_plane, w0_quad)
+        w0_s = deal_scales("w0_s", w0_plane[:])
+        w0_d = deal_words("w0_d", w0_w)
+        xo_g = tile("xo_g", [P, J], U32)
+        nc.vector.tensor_copy(xo_g[:], xo_w[:].indirect(l2[:]))
+        w_s = deal_scales("w_s", spread_within(w_quad))
+        w_d = deal_words("w_d", w_w)
+
+        a_ps = [ps.tile([P, 4, H], F32, name="a_ps%d" % h) for h in range(2)]
+        b_ps = [ps.tile([P, 4, H], F32, name="b_ps%d" % h) for h in range(2)]
+        q_ps = ps.tile([P, 2, J], F32, name="q_ps")
+
+        def cols(h):
+            return slice(h * H, (h + 1) * H)
+
+        for h in range(2):
+            for t in range(4):
+                nc.tensor.matmul_mx(b_ps[h][:, t], lhsT=w2_d[:, t].bitcast(E4M3), lhsT_scale=w2_s[:, t],
+                                    rhs=xo_g[:, cols(h)].bitcast(E5M2), rhs_scale=xo_gs[:, cols(h)], start=True, stop=True)
+        for h in range(2):
+            for t in range(4):
+                nc.tensor.matmul_mx(a_ps[h][:, t], lhsT=w0_d[:, t].bitcast(E4M3), lhsT_scale=w0_s[:, t],
+                                    rhs=xo_g[:, cols(h)].bitcast(E5M2), rhs_scale=xo_gs[:, cols(h)], start=(t == 0), stop=False)
+
+        xt_s = spread_into("xt_s", xt_stage, T, 1)
+        xt_gs = [tile("xt_gs%d" % h, [P, H], U8) for h in range(2)]
+        b_sb = [tile("b_sb0", [P, H, 4], F32, tag="w_w"), tile("b_sb1", [P, H, 4], F32)]
+        for h in range(2):
+            nc.scalar.copy(b_sb[h][:], b_ps[h][:].rearrange("p t j -> p j t"))
+        xt_g = [tile("xt_g%d" % h, [P, H], U16) for h in range(2)]
+        for h in range(2):
+            nc.vector.tensor_copy(xt_gs[h][:], xt_s[:].indirect(l1[:, 8 * h : 8 * h + 8]))
+            nc.vector.tensor_copy(xt_g[h][:], xt_w[:].indirect(l1[:, 8 * h : 8 * h + 8]))
+            for t in range(4):
+                nc.tensor.matmul_mx(a_ps[h][:, t], lhsT=w_d[:, t].bitcast(E5M2), lhsT_scale=w_s[:, t],
+                                    rhs=xt_g[h][:].bitcast(E2M1), rhs_scale=xt_gs[h][:], start=False, stop=(t == 3))
+
+
+        diff = [tile("diff%d" % h, [P, H, 4], F32) for h in range(2)]
+        hid = [tile("hid%d" % h, [P, H * 4], BF16) for h in range(2)]
+        hq = tile("hq", [P, J], U32)
+        hs = tile("hs", [P, J], U8)
+        for h, first, last in ((0, 0, 64), (0, 64, 128), (1, 0, 128)):
+            nc.vector.tensor_tensor(diff[h][:, first:last], a_ps[h][:, :, first:last].rearrange("p t j -> p j t"), b_sb[h][:, first:last], ALU.subtract)
+            nc.scalar.activation(hid[h][:, 4 * first : 4 * last], diff[h][:, first:last].rearrange("p j t -> p (j t)"), ACT.Abs)
+        p_ps = [[ps.tile([P, H], F32, name="p_ps0%d" % u) for u in range(2)],
+                [ps.tile([P, H], F32, name="p_ps1%d" % u, tag="b_ps%d" % u) for u in range(2)]]
+        for h in range(2):
+            nc.vector.quantize_mx(hq[:, cols(h)].bitcast(E5M2), hs[:, cols(h)], hid[h][:])
+            for u in range(2):
+                nc.tensor.matmul_mx(p_ps[h][u][:], lhsT=wb_w[:, cols(u)].bitcast(E4M3), lhsT_scale=wb_s[:, cols(u)],
+                                    rhs=hq[:, cols(h)].bitcast(E5M2), rhs_scale=hs[:, cols(h)], start=True, stop=True)
+        for u in range(2):
+            nc.tensor.matmul_mx(q_ps[:, u], lhsT=wc_w[:, cols(u)].bitcast(E2M1), lhsT_scale=wc_s[:, cols(u)],
+                                rhs=hq[:].bitcast(E5M2), rhs_scale=hs[:], start=True, stop=True)
+
+        p_v = [tile("p_v%d" % h, [P, H], F32) for h in range(2)]
+        p_s = [tile("p_s%d" % h, [P, H], F32) for h in range(2)]
+        for h in range(2):
+            nc.vector.tensor_copy(p_v[h][:], p_ps[h][0][:])
+            nc.scalar.copy(p_s[h][:], p_ps[h][1][:])
+        for h in range(2):
+            nc.vector.tensor_copy(board[0][:].indirect(l3[:, 8 * h : 8 * h + 8]), p_v[h][:])
+            nc.scalar.activation(board[1][:].indirect(l3[:, 8 * h : 8 * h + 8]), p_s[h][:], ACT.Copy)
+
+        q_sb = tile("q_sb", [P, 2, J], F32)
+        nc.vector.tensor_copy(q_sb[:], q_ps[:])
+        q_g = tile("q_g", [P, 2, O], F32)
+        for u in range(2):
+            nc.vector.tensor_copy(q_g[:, u], q_sb[:, u].indirect(l6[:]))
+
+        for u in range(2):
+            gate = tile("gate%d" % u, [P, O], F32)
+            val = tile("val%d" % u, [P, O], F32)
+            prod = tile("prod%d" % u, [P, O], F32)
+            res = tile("res%d" % u, [P, O], F32)
+            nc.scalar.activation(gate[:], board[u][:].indirect(l5[:]), ACT.Sigmoid, bias=bo_c[:, u : u + 1], scale=sp_c[:, u : u + 1])
+            nc.scalar.activation(val[:], board[u][:].indirect(l4[:]), ACT.Copy, scale=so_c[:, u : u + 1])
+            nc.vector.tensor_tensor(prod[:], val[:], gate[:], ALU.mult)
+            nc.vector.tensor_tensor(res[:], prod[:], q_g[:, u], ALU.subtract)
+            nc.sync.dma_start(out[cols(u), :], res[:])

@@ -1,6 +1,7 @@
 from contextlib import ExitStack
 
 import concourse.mybir as mybir
+from concourse.masks import make_identity
 
 K, T, J, R, F, Z, N, C, O = 512, 1024, 256, 512, 512, 1024, 256, 512, 128
 FLOPS = 2 * (3 * 512 * R * J + 2 * R * N * J)
@@ -78,6 +79,20 @@ def tile_list_outcomegatedboard_noted_kernel(
                 nc.vector.tensor_copy(quad[32 * q : 32 * q + 4, 0].bitcast(I32), quad[0:4, q].bitcast(I32))
             return quad[:, 0]
 
+        def upper_tile(name, width):
+            quad = tile(name, [P, 4, width], U8)
+            nc.vector.memset(quad[64:96].bitcast(I32), 0)
+            return quad
+
+        def load_upper(quad, src):
+            rows = src[0].bitcast(I32).rearrange("(q r) c -> r q c", q=4)
+            nc.scalar.dma_start(quad[64:68].bitcast(I32), rows)
+
+        def spread_upper(quad):
+            for q in (0, 1, 3):
+                nc.vector.tensor_copy(quad[32 * q : 32 * q + 32, 2].bitcast(I32), quad[64:96, q].bitcast(I32))
+            return quad[:, 2]
+
         def spread_from(plane, quad):
             for q in range(4):
                 nc.vector.tensor_copy(plane[32 * q : 32 * q + 4].bitcast(I32), quad[:, q].bitcast(I32))
@@ -98,28 +113,26 @@ def tile_list_outcomegatedboard_noted_kernel(
                 nc.sync.dma_start(dst[:], src.rearrange("(u p) o -> p (u o)", p=P))
             return dst
 
-        w_quad = quad_tile("w_quad", R)
+        w0_quad = upper_tile("w0_quad", R)
+        w_quad = upper_tile("w_quad", R)
         xo_s = load_plane("xo_s", xo_scales)
         w2_plane = load_plane("w2_plane", w2_scales)
-        w0_plane = load_plane("w0_plane", w0_scales)
         xt_stage = stage_tile("xt_stage", T, 1)
         wb_s = load_plane("wb_s", wb_scales)
         wc_s = load_plane("wc_s", wc_scales)
-        board = [tile("board%d" % u, [P, C], F32) for u in range(2)]
-        for u in range(2):
-            nc.gpsimd.memset(board[u][:], 0.0)
+        ident = tile("ident", [P, P], F32)
+        make_identity(nc, ident[:])
 
         xo_quad = tile("xo_quad", [4, 4, Z], U8)
         load_quad(xo_quad, xo_scales)
         w2_quad = tile("w2_quad", [4, 4, R], U8)
         load_quad(w2_quad, w2_scales)
-        w0_quad = tile("w0_quad", [4, 4, R], U8)
-        load_quad(w0_quad, w0_scales)
-        load_quad(w_quad, w_scales)
+        load_upper(w0_quad, w0_scales)
+        load_upper(w_quad, w_scales)
         l2 = load_list("l2", offs2)
         l1 = load_list("l1", offs)
-        w2_w = load_words("w2_w", w2_words, R, U32)
         xo_w = load_words("xo_w", xo_words, Z, U32)
+        w2_w = load_words("w2_w", w2_words, R, U32)
         w0_w = load_words("w0_w", w0_words, R, U32)
         w_w = load_words("w_w", w_words, R, U32)
         stage_scales(xt_stage, xt_scales, 1)
@@ -138,57 +151,60 @@ def tile_list_outcomegatedboard_noted_kernel(
 
         spread_from(xo_s, xo_quad)
         spread_from(w2_plane, w2_quad)
-        w2_s = deal_scales("w2_s", w2_plane[:])
-        w2_d = deal_words("w2_d", w2_w)
         xo_gs = tile("xo_gs", [P, J], U8)
         nc.vector.tensor_copy(xo_gs[:], xo_s[:].indirect(l2[:]))
-        spread_from(w0_plane, w0_quad)
-        w0_s = deal_scales("w0_s", w0_plane[:])
-        w0_d = deal_words("w0_d", w0_w)
         xo_g = tile("xo_g", [P, J], U32)
         nc.vector.tensor_copy(xo_g[:], xo_w[:].indirect(l2[:]))
-        w_s = deal_scales("w_s", spread_within(w_quad))
-        w_d = deal_words("w_d", w_w)
+        w0_s = spread_upper(w0_quad)
+        w_s = spread_upper(w_quad)
 
-        a_ps = [ps.tile([P, 4, H], F32, name="a_ps%d" % h) for h in range(2)]
-        b_ps = [ps.tile([P, 4, H], F32, name="b_ps%d" % h) for h in range(2)]
+        a_ps = [ps.tile([P, R], F32, name="a_ps%d" % h) for h in range(2)]
+        b_ps = [ps.tile([P, R], F32, name="b_ps%d" % h) for h in range(2)]
         q_ps = ps.tile([P, 2, J], F32, name="q_ps")
 
         def cols(h):
             return slice(h * H, (h + 1) * H)
 
+        def by_pairs(bank):
+            return bank[:].rearrange("j (p u e) -> j u p e", u=2, e=2)
+
         for h in range(2):
-            for t in range(4):
-                nc.tensor.matmul_mx(b_ps[h][:, t], lhsT=w2_d[:, t].bitcast(E4M3), lhsT_scale=w2_s[:, t],
-                                    rhs=xo_g[:, cols(h)].bitcast(E5M2), rhs_scale=xo_gs[:, cols(h)], start=True, stop=True)
+            nc.tensor.matmul_mx(b_ps[h][:], lhsT=xo_g[:, cols(h)].bitcast(E5M2), lhsT_scale=xo_gs[:, cols(h)],
+                                rhs=w2_w[:].bitcast(E4M3), rhs_scale=w2_plane[:], start=True, stop=True)
         for h in range(2):
-            for t in range(4):
-                nc.tensor.matmul_mx(a_ps[h][:, t], lhsT=w0_d[:, t].bitcast(E4M3), lhsT_scale=w0_s[:, t],
-                                    rhs=xo_g[:, cols(h)].bitcast(E5M2), rhs_scale=xo_gs[:, cols(h)], start=(t == 0), stop=False)
+            nc.tensor.matmul_mx(a_ps[h][:], lhsT=xo_g[:, cols(h)].bitcast(E5M2), lhsT_scale=xo_gs[:, cols(h)],
+                                rhs=w0_w[:].bitcast(E4M3), rhs_scale=w0_s, start=True, stop=False)
 
         xt_s = spread_into("xt_s", xt_stage, T, 1)
         xt_gs = [tile("xt_gs%d" % h, [P, H], U8) for h in range(2)]
-        b_sb = [tile("b_sb0", [P, H, 4], F32, tag="w_w"), tile("b_sb1", [P, H, 4], F32)]
+        b_sb = [tile("b_sb%d" % h, [P, 2, P, 2], F32) for h in range(2)]
         for h in range(2):
-            nc.scalar.copy(b_sb[h][:], b_ps[h][:].rearrange("p t j -> p j t"))
+            nc.scalar.copy(b_sb[h][:], by_pairs(b_ps[h]))
         xt_g = [tile("xt_g%d" % h, [P, H], U16) for h in range(2)]
         for h in range(2):
             nc.vector.tensor_copy(xt_gs[h][:], xt_s[:].indirect(l1[:, 8 * h : 8 * h + 8]))
             nc.vector.tensor_copy(xt_g[h][:], xt_w[:].indirect(l1[:, 8 * h : 8 * h + 8]))
-            for t in range(4):
-                nc.tensor.matmul_mx(a_ps[h][:, t], lhsT=w_d[:, t].bitcast(E5M2), lhsT_scale=w_s[:, t],
-                                    rhs=xt_g[h][:].bitcast(E2M1), rhs_scale=xt_gs[h][:], start=False, stop=(t == 3))
+            nc.tensor.matmul_mx(a_ps[h][:], lhsT=xt_g[h][:].bitcast(E2M1), lhsT_scale=xt_gs[h][:],
+                                rhs=w_w[:].bitcast(E5M2), rhs_scale=w_s, start=False, stop=True)
 
-
-        diff = [tile("diff%d" % h, [P, H, 4], F32) for h in range(2)]
+        diff = [tile("diff%d" % h, [P, 2, P, 2], F32) for h in range(2)]
+        pairs = [tile("pairs%d" % h, [P, 2, P, 2], BF16) for h in range(2)]
         hid = [tile("hid%d" % h, [P, H * 4], BF16) for h in range(2)]
+        t_ps = [ps.tile([P, 2, H], F32, name="t_ps%d" % h, tag="b_ps%d" % h) for h in range(2)]
+        for h in range(2):
+            for u in range(2):
+                nc.vector.tensor_tensor(diff[h][:, u], by_pairs(a_ps[h])[:, u], b_sb[h][:, u], ALU.subtract)
+                nc.scalar.activation(pairs[h][:, u], diff[h][:, u], ACT.Abs)
+                nc.tensor.transpose(t_ps[h][:, u], pairs[h][:, u].rearrange("j p e -> j (p e)").bitcast(F32), ident[:])
+        nc.vector.tensor_copy(hid[0][:].bitcast(F32).rearrange("p (j u) -> p j u", u=2), t_ps[0][:].rearrange("p u j -> p j u"))
+        nc.scalar.copy(hid[1][:].bitcast(F32).rearrange("p (j u) -> p j u", u=2), t_ps[1][:].rearrange("p u j -> p j u"))
+        board = [tile("board%d" % u, [P, C], F32, tag="b_sb%d" % u) for u in range(2)]
+        for u in range(2):
+            nc.gpsimd.memset(board[u][:], 0.0)
         hq = tile("hq", [P, J], U32)
         hs = tile("hs", [P, J], U8)
-        for h, first, last in ((0, 0, 64), (0, 64, 128), (1, 0, 128)):
-            nc.vector.tensor_tensor(diff[h][:, first:last], a_ps[h][:, :, first:last].rearrange("p t j -> p j t"), b_sb[h][:, first:last], ALU.subtract)
-            nc.scalar.activation(hid[h][:, 4 * first : 4 * last], diff[h][:, first:last].rearrange("p j t -> p (j t)"), ACT.Abs)
         p_ps = [[ps.tile([P, H], F32, name="p_ps0%d" % u) for u in range(2)],
-                [ps.tile([P, H], F32, name="p_ps1%d" % u, tag="b_ps%d" % u) for u in range(2)]]
+                [ps.tile([P, H], F32, name="p_ps1%d" % u, tag="a_ps%d" % u) for u in range(2)]]
         for h in range(2):
             nc.vector.quantize_mx(hq[:, cols(h)].bitcast(E5M2), hs[:, cols(h)], hid[h][:])
             for u in range(2):

@@ -70,9 +70,9 @@ def tile_list_outcomegatedboard_noted_kernel(
             for q in range(4):
                 nc.sync.dma_start(plane[32 * q : 32 * q + 4].bitcast(I32), src[0, 4 * q : 4 * q + 4].bitcast(I32))
 
-        def load_quad(quad, src, first=0):
+        def load_quad(queue, quad, src, first=0):
             rows = src[0].bitcast(I32).rearrange("(q r) c -> r q c", q=4)
-            nc.scalar.dma_start(quad[0:4, :, first : first + src.shape[2]].bitcast(I32), rows)
+            queue.dma_start(quad[0:4, :, first : first + src.shape[2]].bitcast(I32), rows)
 
         def spread_within(quad):
             for q in range(1, 4):
@@ -110,37 +110,36 @@ def tile_list_outcomegatedboard_noted_kernel(
         def load_column(name, src):
             dst = tile(name, [P, 2], F32)
             with nc.allow_non_contiguous_dma(reason="one value a partition"):
-                nc.sync.dma_start(dst[:], src.rearrange("(u p) o -> p (u o)", p=P))
+                nc.gpsimd.dma_start(dst[:], src.rearrange("(u p) o -> p (u o)", p=P))
             return dst
 
         w0_quad = upper_tile("w0_quad", R)
-        w_quad = upper_tile("w_quad", R)
+        xt_stage = stage_tile("xt_stage", T, 1)
         xo_s = load_plane("xo_s", xo_scales)
         w2_plane = load_plane("w2_plane", w2_scales)
-        xt_stage = stage_tile("xt_stage", T, 1)
-        wb_s = load_plane("wb_s", wb_scales)
-        wc_s = load_plane("wc_s", wc_scales)
+        w_plane = load_plane("w_plane", w_scales)
+        out_quad = quad_tile("out_quad", 2 * N)
         ident = tile("ident", [P, P], F32)
         make_identity(nc, ident[:])
 
         xo_quad = tile("xo_quad", [4, 4, Z], U8)
-        load_quad(xo_quad, xo_scales)
+        load_quad(nc.scalar, xo_quad, xo_scales)
         w2_quad = tile("w2_quad", [4, 4, R], U8)
-        load_quad(w2_quad, w2_scales)
+        load_quad(nc.scalar, w2_quad, w2_scales)
         load_upper(w0_quad, w0_scales)
-        load_upper(w_quad, w_scales)
         l2 = load_list("l2", offs2)
         l1 = load_list("l1", offs)
         xo_w = load_words("xo_w", xo_words, Z, U32)
         w2_w = load_words("w2_w", w2_words, R, U32)
-        w0_w = load_words("w0_w", w0_words, R, U32)
-        w_w = load_words("w_w", w_words, R, U32)
         stage_scales(xt_stage, xt_scales, 1)
         xt_w = load_words("xt_w", xt_words, T, U16)
-        load_rows(wb_s, wb_scales)
+        w0_w = load_words("w0_w", w0_words, R, U32)
+        w_w = load_words("w_w", w_words, R, U32)
+        load_rows(w_plane, w_scales)
+        load_quad(nc.sync, out_quad, wb_scales)
+        load_quad(nc.sync, out_quad, wc_scales, N)
         wb_w = load_words("wb_w", wb_words, N, U32)
         l3 = load_list("l3", offs3)
-        load_rows(wc_s, wc_scales)
         wc_w = load_words("wc_w", wc_words, N, U16)
         l5 = load_list("l5", offs5)
         l4 = load_list("l4", offs4)
@@ -153,10 +152,10 @@ def tile_list_outcomegatedboard_noted_kernel(
         spread_from(w2_plane, w2_quad)
         xo_gs = tile("xo_gs", [P, J], U8)
         nc.vector.tensor_copy(xo_gs[:], xo_s[:].indirect(l2[:]))
-        xo_g = tile("xo_g", [P, J], U32)
-        nc.vector.tensor_copy(xo_g[:], xo_w[:].indirect(l2[:]))
+        xo_g = [tile("xo_g%d" % h, [P, H], U32) for h in range(2)]
+        for h in range(2):
+            nc.vector.tensor_copy(xo_g[h][:], xo_w[:].indirect(l2[:, 8 * h : 8 * h + 8]))
         w0_s = spread_upper(w0_quad)
-        w_s = spread_upper(w_quad)
 
         a_ps = [ps.tile([P, R], F32, name="a_ps%d" % h) for h in range(2)]
         b_ps = [ps.tile([P, R], F32, name="b_ps%d" % h) for h in range(2)]
@@ -166,18 +165,18 @@ def tile_list_outcomegatedboard_noted_kernel(
             return slice(h * H, (h + 1) * H)
 
         def by_pairs(bank):
-            return bank[:].rearrange("j (p u e) -> j u p e", u=2, e=2)
+            return bank[:].rearrange("j (p t) -> j t p", t=4)
 
         for h in range(2):
-            nc.tensor.matmul_mx(b_ps[h][:], lhsT=xo_g[:, cols(h)].bitcast(E5M2), lhsT_scale=xo_gs[:, cols(h)],
+            nc.tensor.matmul_mx(b_ps[h][:], lhsT=xo_g[h][:].bitcast(E5M2), lhsT_scale=xo_gs[:, cols(h)],
                                 rhs=w2_w[:].bitcast(E4M3), rhs_scale=w2_plane[:], start=True, stop=True)
         for h in range(2):
-            nc.tensor.matmul_mx(a_ps[h][:], lhsT=xo_g[:, cols(h)].bitcast(E5M2), lhsT_scale=xo_gs[:, cols(h)],
+            nc.tensor.matmul_mx(a_ps[h][:], lhsT=xo_g[h][:].bitcast(E5M2), lhsT_scale=xo_gs[:, cols(h)],
                                 rhs=w0_w[:].bitcast(E4M3), rhs_scale=w0_s, start=True, stop=False)
 
         xt_s = spread_into("xt_s", xt_stage, T, 1)
         xt_gs = [tile("xt_gs%d" % h, [P, H], U8) for h in range(2)]
-        b_sb = [tile("b_sb%d" % h, [P, 2, P, 2], F32) for h in range(2)]
+        b_sb = [tile("b_sb%d" % h, [P, 4, P], F32) for h in range(2)]
         for h in range(2):
             nc.scalar.copy(b_sb[h][:], by_pairs(b_ps[h]))
         xt_g = [tile("xt_g%d" % h, [P, H], U16) for h in range(2)]
@@ -185,19 +184,20 @@ def tile_list_outcomegatedboard_noted_kernel(
             nc.vector.tensor_copy(xt_gs[h][:], xt_s[:].indirect(l1[:, 8 * h : 8 * h + 8]))
             nc.vector.tensor_copy(xt_g[h][:], xt_w[:].indirect(l1[:, 8 * h : 8 * h + 8]))
             nc.tensor.matmul_mx(a_ps[h][:], lhsT=xt_g[h][:].bitcast(E2M1), lhsT_scale=xt_gs[h][:],
-                                rhs=w_w[:].bitcast(E5M2), rhs_scale=w_s, start=False, stop=True)
+                                rhs=w_w[:].bitcast(E5M2), rhs_scale=w_plane[:], start=False, stop=True)
 
-        diff = [tile("diff%d" % h, [P, 2, P, 2], F32) for h in range(2)]
-        pairs = [tile("pairs%d" % h, [P, 2, P, 2], BF16) for h in range(2)]
-        hid = [tile("hid%d" % h, [P, H * 4], BF16) for h in range(2)]
-        t_ps = [ps.tile([P, 2, H], F32, name="t_ps%d" % h, tag="b_ps%d" % h) for h in range(2)]
+        diff = [tile("diff%d" % h, [P, 4, P], F32) for h in range(2)]
+        hid = [tile("hid%d" % h, [P, H, 4], BF16) for h in range(2)]
+        t_ps = [ps.tile([P, 4, H], F32, name="t_ps%d" % h, tag="b_ps%d" % h) for h in range(2)]
         for h in range(2):
             for u in range(2):
-                nc.vector.tensor_tensor(diff[h][:, u], by_pairs(a_ps[h])[:, u], b_sb[h][:, u], ALU.subtract)
-                nc.scalar.activation(pairs[h][:, u], diff[h][:, u], ACT.Abs)
-                nc.tensor.transpose(t_ps[h][:, u], pairs[h][:, u].rearrange("j p e -> j (p e)").bitcast(F32), ident[:])
-        nc.vector.tensor_copy(hid[0][:].bitcast(F32).rearrange("p (j u) -> p j u", u=2), t_ps[0][:].rearrange("p u j -> p j u"))
-        nc.scalar.copy(hid[1][:].bitcast(F32).rearrange("p (j u) -> p j u", u=2), t_ps[1][:].rearrange("p u j -> p j u"))
+                two = slice(2 * u, 2 * u + 2)
+                nc.vector.tensor_tensor(diff[h][:, two], by_pairs(a_ps[h])[:, two], b_sb[h][:, two], ALU.subtract)
+                for t in (2 * u, 2 * u + 1):
+                    nc.tensor.transpose(t_ps[h][:, t], diff[h][:, t], ident[:])
+            nc.scalar.activation(hid[h][:], t_ps[h][:].rearrange("p t j -> p j t"), ACT.Abs)
+        out_s = spread_within(out_quad)
+        wb_s, wc_s = out_s[:, 0:N], out_s[:, N : 2 * N]
         board = [tile("board%d" % u, [P, C], F32, tag="b_sb%d" % u) for u in range(2)]
         for u in range(2):
             nc.gpsimd.memset(board[u][:], 0.0)
@@ -206,7 +206,7 @@ def tile_list_outcomegatedboard_noted_kernel(
         p_ps = [[ps.tile([P, H], F32, name="p_ps0%d" % u) for u in range(2)],
                 [ps.tile([P, H], F32, name="p_ps1%d" % u, tag="a_ps%d" % u) for u in range(2)]]
         for h in range(2):
-            nc.vector.quantize_mx(hq[:, cols(h)].bitcast(E5M2), hs[:, cols(h)], hid[h][:])
+            nc.vector.quantize_mx(hq[:, cols(h)].bitcast(E5M2), hs[:, cols(h)], hid[h][:].rearrange("p j t -> p (j t)"))
             for u in range(2):
                 nc.tensor.matmul_mx(p_ps[h][u][:], lhsT=wb_w[:, cols(u)].bitcast(E4M3), lhsT_scale=wb_s[:, cols(u)],
                                     rhs=hq[:, cols(h)].bitcast(E5M2), rhs_scale=hs[:, cols(h)], start=True, stop=True)
@@ -219,7 +219,6 @@ def tile_list_outcomegatedboard_noted_kernel(
         for h in range(2):
             nc.vector.tensor_copy(p_v[h][:], p_ps[h][0][:])
             nc.scalar.copy(p_s[h][:], p_ps[h][1][:])
-        for h in range(2):
             nc.vector.tensor_copy(board[0][:].indirect(l3[:, 8 * h : 8 * h + 8]), p_v[h][:])
             nc.scalar.activation(board[1][:].indirect(l3[:, 8 * h : 8 * h + 8]), p_s[h][:], ACT.Copy)
 

@@ -70,9 +70,9 @@ def tile_list_outcomegatedboard_noted_kernel(
             for q in range(4):
                 nc.sync.dma_start(plane[32 * q : 32 * q + 4].bitcast(I32), src[0, 4 * q : 4 * q + 4].bitcast(I32))
 
-        def load_quad(queue, quad, src, first=0):
+        def load_quad(quad, src, first=0):
             rows = src[0].bitcast(I32).rearrange("(q r) c -> r q c", q=4)
-            queue.dma_start(quad[0:4, :, first : first + src.shape[2]].bitcast(I32), rows)
+            nc.scalar.dma_start(quad[0:4, :, first : first + src.shape[2]].bitcast(I32), rows)
 
         def spread_within(quad):
             for q in range(1, 4):
@@ -110,36 +110,40 @@ def tile_list_outcomegatedboard_noted_kernel(
         def load_column(name, src):
             dst = tile(name, [P, 2], F32)
             with nc.allow_non_contiguous_dma(reason="one value a partition"):
-                nc.gpsimd.dma_start(dst[:], src.rearrange("(u p) o -> p (u o)", p=P))
+                nc.sync.dma_start(dst[:], src.rearrange("(u p) o -> p (u o)", p=P))
             return dst
 
         w0_quad = upper_tile("w0_quad", R)
-        xt_stage = stage_tile("xt_stage", T, 1)
+        w_quad = upper_tile("w_quad", R)
         xo_s = load_plane("xo_s", xo_scales)
         w2_plane = load_plane("w2_plane", w2_scales)
-        w_plane = load_plane("w_plane", w_scales)
-        out_quad = quad_tile("out_quad", 2 * N)
+        xt_stage = stage_tile("xt_stage", T, 1)
+        wb_s = load_plane("wb_s", wb_scales)
+        wc_s = load_plane("wc_s", wc_scales)
         ident = tile("ident", [P, P], F32)
         make_identity(nc, ident[:])
 
         xo_quad = tile("xo_quad", [4, 4, Z], U8)
-        load_quad(nc.scalar, xo_quad, xo_scales)
+        load_quad(xo_quad, xo_scales)
         w2_quad = tile("w2_quad", [4, 4, R], U8)
-        load_quad(nc.scalar, w2_quad, w2_scales)
+        load_quad(w2_quad, w2_scales)
         load_upper(w0_quad, w0_scales)
+        load_upper(w_quad, w_scales)
+        warm = tile("warm", [P, 2], F32)
+        nc.vector.memset(warm[:, 0:1], 0.0)
+        nc.scalar.activation(warm[:, 1:2], warm[:, 0:1], ACT.Sigmoid)
         l2 = load_list("l2", offs2)
         l1 = load_list("l1", offs)
         xo_w = load_words("xo_w", xo_words, Z, U32)
         w2_w = load_words("w2_w", w2_words, R, U32)
-        stage_scales(xt_stage, xt_scales, 1)
-        xt_w = load_words("xt_w", xt_words, T, U16)
         w0_w = load_words("w0_w", w0_words, R, U32)
         w_w = load_words("w_w", w_words, R, U32)
-        load_rows(w_plane, w_scales)
-        load_quad(nc.sync, out_quad, wb_scales)
-        load_quad(nc.sync, out_quad, wc_scales, N)
+        stage_scales(xt_stage, xt_scales, 1)
+        xt_w = load_words("xt_w", xt_words, T, U16)
+        load_rows(wb_s, wb_scales)
         wb_w = load_words("wb_w", wb_words, N, U32)
         l3 = load_list("l3", offs3)
+        load_rows(wc_s, wc_scales)
         wc_w = load_words("wc_w", wc_words, N, U16)
         l5 = load_list("l5", offs5)
         l4 = load_list("l4", offs4)
@@ -152,10 +156,10 @@ def tile_list_outcomegatedboard_noted_kernel(
         spread_from(w2_plane, w2_quad)
         xo_gs = tile("xo_gs", [P, J], U8)
         nc.vector.tensor_copy(xo_gs[:], xo_s[:].indirect(l2[:]))
-        xo_g = [tile("xo_g%d" % h, [P, H], U32) for h in range(2)]
-        for h in range(2):
-            nc.vector.tensor_copy(xo_g[h][:], xo_w[:].indirect(l2[:, 8 * h : 8 * h + 8]))
+        xo_g = tile("xo_g", [P, J], U32)
+        nc.vector.tensor_copy(xo_g[:], xo_w[:].indirect(l2[:]))
         w0_s = spread_upper(w0_quad)
+        w_s = spread_upper(w_quad)
 
         a_ps = [ps.tile([P, R], F32, name="a_ps%d" % h) for h in range(2)]
         b_ps = [ps.tile([P, R], F32, name="b_ps%d" % h) for h in range(2)]
@@ -165,18 +169,18 @@ def tile_list_outcomegatedboard_noted_kernel(
             return slice(h * H, (h + 1) * H)
 
         def by_pairs(bank):
-            return bank[:].rearrange("j (p t) -> j t p", t=4)
+            return bank[:].rearrange("j (p u e) -> j u p e", u=2, e=2)
 
         for h in range(2):
-            nc.tensor.matmul_mx(b_ps[h][:], lhsT=xo_g[h][:].bitcast(E5M2), lhsT_scale=xo_gs[:, cols(h)],
+            nc.tensor.matmul_mx(b_ps[h][:], lhsT=xo_g[:, cols(h)].bitcast(E5M2), lhsT_scale=xo_gs[:, cols(h)],
                                 rhs=w2_w[:].bitcast(E4M3), rhs_scale=w2_plane[:], start=True, stop=True)
         for h in range(2):
-            nc.tensor.matmul_mx(a_ps[h][:], lhsT=xo_g[h][:].bitcast(E5M2), lhsT_scale=xo_gs[:, cols(h)],
+            nc.tensor.matmul_mx(a_ps[h][:], lhsT=xo_g[:, cols(h)].bitcast(E5M2), lhsT_scale=xo_gs[:, cols(h)],
                                 rhs=w0_w[:].bitcast(E4M3), rhs_scale=w0_s, start=True, stop=False)
 
         xt_s = spread_into("xt_s", xt_stage, T, 1)
         xt_gs = [tile("xt_gs%d" % h, [P, H], U8) for h in range(2)]
-        b_sb = [tile("b_sb%d" % h, [P, 4, P], F32) for h in range(2)]
+        b_sb = [tile("b_sb%d" % h, [P, 2, P, 2], F32) for h in range(2)]
         for h in range(2):
             nc.scalar.copy(b_sb[h][:], by_pairs(b_ps[h]))
         xt_g = [tile("xt_g%d" % h, [P, H], U16) for h in range(2)]
@@ -184,20 +188,19 @@ def tile_list_outcomegatedboard_noted_kernel(
             nc.vector.tensor_copy(xt_gs[h][:], xt_s[:].indirect(l1[:, 8 * h : 8 * h + 8]))
             nc.vector.tensor_copy(xt_g[h][:], xt_w[:].indirect(l1[:, 8 * h : 8 * h + 8]))
             nc.tensor.matmul_mx(a_ps[h][:], lhsT=xt_g[h][:].bitcast(E2M1), lhsT_scale=xt_gs[h][:],
-                                rhs=w_w[:].bitcast(E5M2), rhs_scale=w_plane[:], start=False, stop=True)
+                                rhs=w_w[:].bitcast(E5M2), rhs_scale=w_s, start=False, stop=True)
 
-        diff = [tile("diff%d" % h, [P, 4, P], F32) for h in range(2)]
-        hid = [tile("hid%d" % h, [P, H, 4], BF16) for h in range(2)]
-        t_ps = [ps.tile([P, 4, H], F32, name="t_ps%d" % h, tag="b_ps%d" % h) for h in range(2)]
+        diff = [tile("diff%d" % h, [P, 2, P, 2], F32) for h in range(2)]
+        pairs = [tile("pairs%d" % h, [P, 2, P, 2], BF16) for h in range(2)]
+        hid = [tile("hid%d" % h, [P, H * 4], BF16) for h in range(2)]
+        t_ps = [ps.tile([P, 2, H], F32, name="t_ps%d" % h, tag="b_ps%d" % h) for h in range(2)]
         for h in range(2):
             for u in range(2):
-                two = slice(2 * u, 2 * u + 2)
-                nc.vector.tensor_tensor(diff[h][:, two], by_pairs(a_ps[h])[:, two], b_sb[h][:, two], ALU.subtract)
-                for t in (2 * u, 2 * u + 1):
-                    nc.tensor.transpose(t_ps[h][:, t], diff[h][:, t], ident[:])
-            nc.scalar.activation(hid[h][:], t_ps[h][:].rearrange("p t j -> p j t"), ACT.Abs)
-        out_s = spread_within(out_quad)
-        wb_s, wc_s = out_s[:, 0:N], out_s[:, N : 2 * N]
+                nc.vector.tensor_tensor(diff[h][:, u], by_pairs(a_ps[h])[:, u], b_sb[h][:, u], ALU.subtract)
+                nc.scalar.activation(pairs[h][:, u], diff[h][:, u], ACT.Abs)
+                nc.tensor.transpose(t_ps[h][:, u], pairs[h][:, u].rearrange("j p e -> j (p e)").bitcast(F32), ident[:])
+        nc.vector.tensor_copy(hid[0][:].bitcast(F32).rearrange("p (j u) -> p j u", u=2), t_ps[0][:].rearrange("p u j -> p j u"))
+        nc.scalar.copy(hid[1][:].bitcast(F32).rearrange("p (j u) -> p j u", u=2), t_ps[1][:].rearrange("p u j -> p j u"))
         board = [tile("board%d" % u, [P, C], F32, tag="b_sb%d" % u) for u in range(2)]
         for u in range(2):
             nc.gpsimd.memset(board[u][:], 0.0)
@@ -206,7 +209,7 @@ def tile_list_outcomegatedboard_noted_kernel(
         p_ps = [[ps.tile([P, H], F32, name="p_ps0%d" % u) for u in range(2)],
                 [ps.tile([P, H], F32, name="p_ps1%d" % u, tag="a_ps%d" % u) for u in range(2)]]
         for h in range(2):
-            nc.vector.quantize_mx(hq[:, cols(h)].bitcast(E5M2), hs[:, cols(h)], hid[h][:].rearrange("p j t -> p (j t)"))
+            nc.vector.quantize_mx(hq[:, cols(h)].bitcast(E5M2), hs[:, cols(h)], hid[h][:])
             for u in range(2):
                 nc.tensor.matmul_mx(p_ps[h][u][:], lhsT=wb_w[:, cols(u)].bitcast(E4M3), lhsT_scale=wb_s[:, cols(u)],
                                     rhs=hq[:, cols(h)].bitcast(E5M2), rhs_scale=hs[:, cols(h)], start=True, stop=True)
@@ -219,6 +222,7 @@ def tile_list_outcomegatedboard_noted_kernel(
         for h in range(2):
             nc.vector.tensor_copy(p_v[h][:], p_ps[h][0][:])
             nc.scalar.copy(p_s[h][:], p_ps[h][1][:])
+        for h in range(2):
             nc.vector.tensor_copy(board[0][:].indirect(l3[:, 8 * h : 8 * h + 8]), p_v[h][:])
             nc.scalar.activation(board[1][:].indirect(l3[:, 8 * h : 8 * h + 8]), p_s[h][:], ACT.Copy)
 

from contextlib import ExitStack

import concourse.mybir as mybir
from concourse.masks import make_identity

K, T, J, R, F, Z, N, C, O = 512, 1024, 256, 512, 512, 1024, 256, 512, 128
FLOPS = 2 * (3 * 512 * R * J + 2 * R * N * J)

F32, BF16 = mybir.dt.float32, mybir.dt.bfloat16
I32, U32, U16, U8 = mybir.dt.int32, mybir.dt.uint32, mybir.dt.uint16, mybir.dt.uint8
E4M3, E5M2, E2M1 = mybir.dt.float8_e4m3fn_x4, mybir.dt.float8_e5m2_x4, mybir.dt.float4_e2m1fn_x4
ACT = mybir.ActivationFunctionType
ALU = mybir.AluOpType
P = 128
H = 128


def tile_list_outcomegatedboard_noted_kernel(
    tc, xt_words, xt_scales, xo_words, xo_scales, w_words, w_scales, w0_words, w0_scales, w2_words, w2_scales,
    wb_words, wb_scales, wc_words, wc_scales, so, sp, bo, offs, offs2, offs3, offs4, offs5, offs6, out,
):
    nc = tc.nc
    with ExitStack() as ctx:
        lists = ctx.enter_context(tc.tile_pool(name="lists", bufs=1))
        sb = ctx.enter_context(tc.tile_pool(name="sb", bufs=1))
        ps = ctx.enter_context(tc.psum_pool(name="ps", bufs=1))

        def tile(name, shape, dtype, tag=None):
            return sb.tile(shape, dtype, name=name, tag=tag or name, align_bytes=64)

        def load_list(name, src):
            dst = lists.tile(list(src.shape), U16, name=name)
            nc.sync.dma_start(dst[:], src)
            return dst

        def load_words(name, src, width, dtype):
            dst = tile(name, [P, width], dtype)
            flat = src[0] if src.ndim == 3 else src[0].rearrange("p c r -> p (c r)")
            nc.sync.dma_start(dst[:].bitcast(I32), flat.bitcast(I32))
            return dst

        def stage_tile(name, width, half):
            stage = tile(name, [P, 2, width], U8)
            nc.vector.memset(stage[64 * half : 64 * half + 64].bitcast(I32), 0)
            return stage

        def stage_scales(stage, src, half):
            rows = src[0].bitcast(I32).rearrange("(h g r) c -> g r h c", h=2, g=2)
            for g in range(2):
                first = 64 * half + 32 * g
                nc.sync.dma_start(stage[first : first + 4].bitcast(I32), rows[g])

        def spread_into(name, stage, width, half):
            plane = tile(name, [P, width], U8)
            for h in range(2):
                nc.vector.tensor_copy(plane[64 * h : 64 * h + 64].bitcast(I32), stage[64 * half : 64 * half + 64, h].bitcast(I32))
            return plane

        def quad_tile(name, width):
            quad = tile(name, [P, 4, width], U8)
            nc.vector.memset(quad[:, 0].bitcast(I32), 0)
            return quad

        def load_plane(name, src):
            plane = tile(name, [P, src.shape[2]], U8)
            nc.vector.memset(plane[:].bitcast(I32), 0)
            return plane

        def load_rows(plane, src):
            for q in range(4):
                nc.sync.dma_start(plane[32 * q : 32 * q + 4].bitcast(I32), src[0, 4 * q : 4 * q + 4].bitcast(I32))

        def load_quad(quad, src, first=0):
            rows = src[0].bitcast(I32).rearrange("(q r) c -> r q c", q=4)
            nc.scalar.dma_start(quad[0:4, :, first : first + src.shape[2]].bitcast(I32), rows)

        def spread_within(quad):
            for q in range(1, 4):
                nc.vector.tensor_copy(quad[32 * q : 32 * q + 4, 0].bitcast(I32), quad[0:4, q].bitcast(I32))
            return quad[:, 0]

        def upper_tile(name, width):
            quad = tile(name, [P, 4, width], U8)
            nc.vector.memset(quad[64:96].bitcast(I32), 0)
            return quad

        def load_upper(quad, src):
            rows = src[0].bitcast(I32).rearrange("(q r) c -> r q c", q=4)
            nc.scalar.dma_start(quad[64:68].bitcast(I32), rows)

        def spread_upper(quad):
            for q in (0, 1, 3):
                nc.vector.tensor_copy(quad[32 * q : 32 * q + 32, 2].bitcast(I32), quad[64:96, q].bitcast(I32))
            return quad[:, 2]

        def spread_from(plane, quad):
            for q in range(4):
                nc.vector.tensor_copy(plane[32 * q : 32 * q + 4].bitcast(I32), quad[:, q].bitcast(I32))

        def deal_scales(name, plane):
            dealt = tile(name, [P, 4, P], U8)
            nc.gpsimd.tensor_copy(dealt[:], plane.rearrange("p (m t) -> p t m", t=4))
            return dealt

        def deal_words(name, words):
            dealt = tile(name, [P, 4, P], U32)
            nc.scalar.copy(dealt[:].rearrange("p t m -> p m t"), words[:].rearrange("p (m t) -> p m t", t=4))
            return dealt

        def load_column(name, src):
            dst = tile(name, [P, 2], F32)
            with nc.allow_non_contiguous_dma(reason="one value a partition"):
                nc.sync.dma_start(dst[:], src.rearrange("(u p) o -> p (u o)", p=P))
            return dst

        w0_quad = upper_tile("w0_quad", R)
        w_quad = upper_tile("w_quad", R)
        xo_s = load_plane("xo_s", xo_scales)
        w2_plane = load_plane("w2_plane", w2_scales)
        xt_stage = stage_tile("xt_stage", T, 1)
        wb_s = load_plane("wb_s", wb_scales)
        wc_s = load_plane("wc_s", wc_scales)
        ident = tile("ident", [P, P], F32)
        make_identity(nc, ident[:])

        xo_quad = tile("xo_quad", [4, 4, Z], U8)
        load_quad(xo_quad, xo_scales)
        w2_quad = tile("w2_quad", [4, 4, R], U8)
        load_quad(w2_quad, w2_scales)
        load_upper(w0_quad, w0_scales)
        load_upper(w_quad, w_scales)
        warm = tile("warm", [P, 2], F32)
        nc.vector.memset(warm[:, 0:1], 0.0)
        nc.scalar.activation(warm[:, 1:2], warm[:, 0:1], ACT.Sigmoid)
        l2 = load_list("l2", offs2)
        l1 = load_list("l1", offs)
        xo_w = load_words("xo_w", xo_words, Z, U32)
        w2_w = load_words("w2_w", w2_words, R, U32)
        w0_w = load_words("w0_w", w0_words, R, U32)
        w_w = load_words("w_w", w_words, R, U32)
        stage_scales(xt_stage, xt_scales, 1)
        xt_w = load_words("xt_w", xt_words, T, U16)
        load_rows(wb_s, wb_scales)
        wb_w = load_words("wb_w", wb_words, N, U32)
        l3 = load_list("l3", offs3)
        load_rows(wc_s, wc_scales)
        wc_w = load_words("wc_w", wc_words, N, U16)
        l5 = load_list("l5", offs5)
        l4 = load_list("l4", offs4)
        l6 = load_list("l6", offs6)
        sp_c = load_column("sp_c", sp)
        bo_c = load_column("bo_c", bo)
        so_c = load_column("so_c", so)

        spread_from(xo_s, xo_quad)
        spread_from(w2_plane, w2_quad)
        xo_gs = tile("xo_gs", [P, J], U8)
        nc.vector.tensor_copy(xo_gs[:], xo_s[:].indirect(l2[:]))
        xo_g = tile("xo_g", [P, J], U32)
        nc.vector.tensor_copy(xo_g[:], xo_w[:].indirect(l2[:]))
        w0_s = spread_upper(w0_quad)
        w_s = spread_upper(w_quad)

        a_ps = [ps.tile([P, R], F32, name="a_ps%d" % h) for h in range(2)]
        b_ps = [ps.tile([P, R], F32, name="b_ps%d" % h) for h in range(2)]
        q_ps = ps.tile([P, 2, J], F32, name="q_ps")

        def cols(h):
            return slice(h * H, (h + 1) * H)

        def by_pairs(bank):
            return bank[:].rearrange("j (p u e) -> j u p e", u=2, e=2)

        for h in range(2):
            nc.tensor.matmul_mx(b_ps[h][:], lhsT=xo_g[:, cols(h)].bitcast(E5M2), lhsT_scale=xo_gs[:, cols(h)],
                                rhs=w2_w[:].bitcast(E4M3), rhs_scale=w2_plane[:], start=True, stop=True)
        for h in range(2):
            nc.tensor.matmul_mx(a_ps[h][:], lhsT=xo_g[:, cols(h)].bitcast(E5M2), lhsT_scale=xo_gs[:, cols(h)],
                                rhs=w0_w[:].bitcast(E4M3), rhs_scale=w0_s, start=True, stop=False)

        xt_s = spread_into("xt_s", xt_stage, T, 1)
        xt_gs = [tile("xt_gs%d" % h, [P, H], U8) for h in range(2)]
        b_sb = [tile("b_sb%d" % h, [P, 2, P, 2], F32) for h in range(2)]
        for h in range(2):
            nc.scalar.copy(b_sb[h][:], by_pairs(b_ps[h]))
        xt_g = [tile("xt_g%d" % h, [P, H], U16) for h in range(2)]
        for h in range(2):
            nc.vector.tensor_copy(xt_gs[h][:], xt_s[:].indirect(l1[:, 8 * h : 8 * h + 8]))
            nc.vector.tensor_copy(xt_g[h][:], xt_w[:].indirect(l1[:, 8 * h : 8 * h + 8]))
            nc.tensor.matmul_mx(a_ps[h][:], lhsT=xt_g[h][:].bitcast(E2M1), lhsT_scale=xt_gs[h][:],
                                rhs=w_w[:].bitcast(E5M2), rhs_scale=w_s, start=False, stop=True)

        diff = [tile("diff%d" % h, [P, 2, P, 2], F32) for h in range(2)]
        pairs = [tile("pairs%d" % h, [P, 2, P, 2], BF16) for h in range(2)]
        hid = [tile("hid%d" % h, [P, H * 4], BF16) for h in range(2)]
        t_ps = [ps.tile([P, 2, H], F32, name="t_ps%d" % h, tag="b_ps%d" % h) for h in range(2)]
        for h in range(2):
            for u in range(2):
                nc.vector.tensor_tensor(diff[h][:, u], by_pairs(a_ps[h])[:, u], b_sb[h][:, u], ALU.subtract)
                nc.scalar.activation(pairs[h][:, u], diff[h][:, u], ACT.Abs)
                nc.tensor.transpose(t_ps[h][:, u], pairs[h][:, u].rearrange("j p e -> j (p e)").bitcast(F32), ident[:])
        nc.vector.tensor_copy(hid[0][:].bitcast(F32).rearrange("p (j u) -> p j u", u=2), t_ps[0][:].rearrange("p u j -> p j u"))
        nc.scalar.copy(hid[1][:].bitcast(F32).rearrange("p (j u) -> p j u", u=2), t_ps[1][:].rearrange("p u j -> p j u"))
        board = [tile("board%d" % u, [P, C], F32, tag="b_sb%d" % u) for u in range(2)]
        for u in range(2):
            nc.gpsimd.memset(board[u][:], 0.0)
        hq = tile("hq", [P, J], U32)
        hs = tile("hs", [P, J], U8)
        p_ps = [[ps.tile([P, H], F32, name="p_ps0%d" % u) for u in range(2)],
                [ps.tile([P, H], F32, name="p_ps1%d" % u, tag="a_ps%d" % u) for u in range(2)]]
        for h in range(2):
            nc.vector.quantize_mx(hq[:, cols(h)].bitcast(E5M2), hs[:, cols(h)], hid[h][:])
            for u in range(2):
                nc.tensor.matmul_mx(p_ps[h][u][:], lhsT=wb_w[:, cols(u)].bitcast(E4M3), lhsT_scale=wb_s[:, cols(u)],
                                    rhs=hq[:, cols(h)].bitcast(E5M2), rhs_scale=hs[:, cols(h)], start=True, stop=True)
        for u in range(2):
            nc.tensor.matmul_mx(q_ps[:, u], lhsT=wc_w[:, cols(u)].bitcast(E2M1), lhsT_scale=wc_s[:, cols(u)],
                                rhs=hq[:].bitcast(E5M2), rhs_scale=hs[:], start=True, stop=True)

        p_v = [tile("p_v%d" % h, [P, H], F32) for h in range(2)]
        p_s = [tile("p_s%d" % h, [P, H], F32) for h in range(2)]
        for h in range(2):
            nc.vector.tensor_copy(p_v[h][:], p_ps[h][0][:])
            nc.scalar.copy(p_s[h][:], p_ps[h][1][:])
        for h in range(2):
            nc.vector.tensor_copy(board[0][:].indirect(l3[:, 8 * h : 8 * h + 8]), p_v[h][:])
            nc.scalar.activation(board[1][:].indirect(l3[:, 8 * h : 8 * h + 8]), p_s[h][:], ACT.Copy)

        q_sb = tile("q_sb", [P, 2, J], F32)
        nc.vector.tensor_copy(q_sb[:], q_ps[:])
        q_g = tile("q_g", [P, 2, O], F32)
        for u in range(2):
            nc.vector.tensor_copy(q_g[:, u], q_sb[:, u].indirect(l6[:]))

        for u in range(2):
            gate = tile("gate%d" % u, [P, O], F32)
            val = tile("val%d" % u, [P, O], F32)
            prod = tile("prod%d" % u, [P, O], F32)
            res = tile("res%d" % u, [P, O], F32)
            nc.scalar.activation(gate[:], board[u][:].indirect(l5[:]), ACT.Sigmoid, bias=bo_c[:, u : u + 1], scale=sp_c[:, u : u + 1])
            nc.scalar.activation(val[:], board[u][:].indirect(l4[:]), ACT.Copy, scale=so_c[:, u : u + 1])
            nc.vector.tensor_tensor(prod[:], val[:], gate[:], ALU.mult)
            nc.vector.tensor_tensor(res[:], prod[:], q_g[:, u], ALU.subtract)
            nc.sync.dma_start(out[cols(u), :], res[:])
